import numpy as np
import ml_dtypes


def mxq(x, axis, fmt="e4m3"):
    dtype, down = {"e4m3": (ml_dtypes.float8_e4m3fn, 7), "e5m2": (ml_dtypes.float8_e5m2, 14)}[fmt]
    v = np.moveaxis(np.asarray(x, np.float32).astype(ml_dtypes.bfloat16).astype(np.float64), axis, -1)
    blocks = v.reshape(v.shape[:-1] + (-1, 32))
    amax = np.abs(blocks).max(-1, keepdims=True)
    byte = np.maximum(np.where(amax > 0, np.frexp(amax)[1] - 1 + 127, 0) - down, 1)
    scale = np.exp2(byte - 127.0)
    codes = (blocks / scale).astype(np.float32).astype(dtype).astype(np.float64)
    return np.moveaxis((codes * scale).reshape(v.shape), -1, axis)


WIDE = False


def mx_kscale(k):
    if not WIDE:
        return np.ones(k)
    levels = np.array([10, -10, 5, -5, 0])
    if k % 512:
        return np.exp2(np.random.permutation(np.resize(levels, k // 32))).repeat(32)
    a = np.empty((k // 512, 16))
    for p in range(k // 512):
        a[p, :8] = np.random.permutation(np.resize(levels, 8))
        for g in range(8):
            far = levels[np.abs(levels - a[p, g]) >= 10]
            a[p, g + 8] = far[np.random.randint(len(far))]
    return np.exp2(a.ravel()).repeat(32)


BF16 = ml_dtypes.bfloat16


def bf(x):
    return np.asarray(x, np.float32).astype(BF16)


def f64(x):
    return np.asarray(x).astype(np.float64)


E2M1 = np.array([0.0, 0.5, 1.0, 1.5, 2.0, 3.0, 4.0, 6.0, -0.0, -0.5, -1.0, -1.5, -2.0, -3.0, -4.0, -6.0])


def pack_weight(w, fmt):
    k, n = w.shape
    w = f64(bf(w)).reshape(k // 32, 32, n)
    amax = np.abs(w).max(1)
    if fmt == "e4m3":
        byte = np.frexp(amax)[1] - 1 + 127 - 7
    else:
        mant, ex = np.frexp(amax / 6.0)
        byte = np.where(mant > 0.5, ex, ex - 1) + 127
    byte = np.clip(np.where(amax > 0, byte, 1), 1, 254)
    scaled = (w * np.exp2(127.0 - byte)[:, None, :]).reshape(k, n).astype(np.float32)
    by_word = np.ascontiguousarray(scaled.reshape(k // 512, 128, 4, n).transpose(0, 1, 3, 2))
    if fmt == "e4m3":
        words = by_word.astype(ml_dtypes.float8_e4m3fn).view(np.uint8)
    else:
        c = by_word.astype(ml_dtypes.float4_e2m1fn).view(np.uint8) & 0xF
        words = c[..., 0::2] | (c[..., 1::2] << 4)
    return np.ascontiguousarray(words), np.ascontiguousarray(byte.astype(np.uint8).reshape(k // 512, 16, n))


def unpack_weight(words, scales, fmt):
    g, p, n, _ = words.shape
    if fmt == "e4m3":
        vals = np.ascontiguousarray(words).view(ml_dtypes.float8_e4m3fn).astype(np.float64)
    else:
        nib = np.empty((g, p, n, 4), np.uint8)
        nib[..., 0::2] = words & 0xF
        nib[..., 1::2] = words >> 4
        vals = E2M1[nib]
    vals = vals * np.repeat(np.exp2(scales.astype(np.float64) - 127.0), 8, axis=1)[..., None]
    return vals.transpose(0, 1, 3, 2).reshape(g * 512, n)
def pack4(w):
    words, scales = pack_weight(w, "e2m1")
    return words.reshape(words.shape[0], 128, -1), scales


def unpack4(words, scales):
    return unpack_weight(words.reshape(words.shape[0], 128, -1, 2), scales, "e2m1")


def planes(Y):
    n, m = Y.shape
    b = f64(bf(Y)).reshape(n // 32, 32, m)
    amax = np.abs(b).max(1)
    byte = np.clip(np.where(amax > 0, np.frexp(amax)[1] - 1 + 127 - 7, 1), 1, 254)
    codes = (b * np.exp2(127.0 - byte)[:, None, :]).reshape(n, m).astype(np.float32).astype(ml_dtypes.float8_e4m3fn).view(np.uint8)
    words = codes.reshape(n // 512, 128, 4, m).transpose(0, 1, 3, 2)
    return np.ascontiguousarray(words), np.ascontiguousarray(byte.astype(np.uint8).reshape(n // 512, 16, m))


T, D, M = 1024, 1024, 1024
Z = D + M


def transform_factors(z, w, s, b):
    p = mxq(z, 1, "e4m3") @ w
    return z + np.maximum(s[None, :] * p + b[None, :], 0.0)


def setup_inputs():
    k, t = mx_kscale(Z), mx_kscale(T)
    u = bf(np.random.standard_normal((T, D)) * k[:D])
    d = bf(np.random.standard_normal((T, M)) * k[D:])
    w_words, w_scales = pack4(np.random.standard_normal((Z, Z)) / np.sqrt(Z) / k[:, None])
    return {
        "u": u,
        "d": d,
        "w_words": w_words,
        "w_scales": w_scales,
        "s": bf((1.0 + 0.1 * np.random.standard_normal(Z)) * k),
        "b": bf(np.random.standard_normal(Z) * 0.3 * k),
        "a": bf(np.random.standard_normal(T) * t),
        "c": bf((1.0 + 0.1 * np.random.standard_normal(T)) / t),
    }


def core(u, d, w_words, w_scales, s, b, a, c):
    n_tokens, d_in = u.shape
    z = np.concatenate([f64(u), f64(d)], axis=-1)
    h = transform_factors(z, unpack4(w_words, w_scales), f64(s), f64(b))
    ut = h[:, :d_in] * f64(a)[:, None]
    dt = h[:, d_in:] * f64(c)[:, None]
    return (mxq(ut, 0, "e4m3").T @ mxq(dt, 0, "e4m3")) / np.sqrt(n_tokens)


def reference(u, d, w_words, w_scales, s, b, a, c):
    R_out = core(u, d, w_words, w_scales, s, b, a, c)
    words, scales = planes(R_out.T)
    return R_out, words, scales

from contextlib import ExitStack

import concourse.mybir as mybir
from concourse.masks import make_identity

F32 = mybir.dt.float32
BF16 = mybir.dt.bfloat16
I32 = mybir.dt.int32
U32 = mybir.dt.uint32
U8 = mybir.dt.uint8
FP8X4 = mybir.dt.float8_e4m3fn_x4
FP4X4 = mybir.dt.float4_e2m1fn_x4
ACT = mybir.ActivationFunctionType
ALU = mybir.AluOpType

T, D, M = 1024, 1024, 1024
Z = D + M
P = 128
FLOPS = 2 * T * Z * Z + 2 * T * D * M


def tile_mendgradienttransformweightedit_x2_kernel(tc, u, d, w_words, w_scales, s, b, a, c, out_0, out_1, out_2):
    nc = tc.nc
    with ExitStack() as ctx:
        keep = ctx.enter_context(tc.tile_pool(name="keep", bufs=1))
        work = ctx.enter_context(tc.tile_pool(name="work", bufs=3))
        psum = ctx.enter_context(tc.psum_pool(name="psum", bufs=4))
        ctx.enter_context(tc.manual_schedule())

        wsc = keep.tile([P, 4 * Z], U8, name="wsc", align_bytes=64)
        nc.vector.memset(wsc[:].bitcast(I32), 0)
        rows = keep.tile([P, P], BF16, name="rows")
        nc.vector.memset(rows[:], 0.0)
        identb = keep.tile([P, P], BF16, name="identb")
        make_identity(nc, identb[:])
        ident = keep.tile([P, P], F32, name="ident")
        nc.scalar.copy(out=ident[:], in_=identb[:])

        zr = [[keep.tile([P, 4, 512], BF16, name="zr%d%d" % (g, k)) for k in range(4)] for g in range(2)]
        wt = [keep.tile([P, 4, 1024], U8, name="wt%d" % cb, align_bytes=64) for cb in range(4)]

        def load_z(g, k):
            src = (u, d)[k // 2]
            col = 512 * (k % 2)
            nc.sync.dma_start(
                out=zr[g][k][:],
                in_=src[512 * g : 512 * (g + 1), col : col + 512].rearrange("(p t) k -> p t k", t=4),
            )

        def load_w(cb):
            nc.sync.dma_start(
                out=wt[cb][:].bitcast(I32),
                in_=w_words[:, :, 1024 * cb : 1024 * (cb + 1)].bitcast(I32).rearrange("g p n -> p g n"),
            )

        load_z(0, 0)
        load_w(2)
        for q in range(4):
            nc.sync.dma_start(
                out=wsc[32 * q : 32 * q + 4, :].bitcast(I32).rearrange("r (g n) -> r g n", g=4),
                in_=w_scales[:, 4 * q : 4 * q + 4, :].bitcast(I32).rearrange("g r n -> r g n"),
            )
        load_z(0, 1)
        load_z(0, 2)
        load_z(0, 3)
        load_w(3)
        for k in range(4):
            load_z(1, k)
        load_w(0)
        load_w(1)

        ac = [keep.tile([P, 2, 4], BF16, name="ac%d" % i) for i in range(2)]
        nc.scalar.dma_start(out=rows[0:16, :], in_=s.rearrange("(j q) -> j q", q=P))
        nc.scalar.dma_start(out=rows[16:32, :], in_=b.rearrange("(j q) -> j q", q=P))
        nc.scalar.dma_start(out=ac[0][:], in_=a.rearrange("(g p t) -> p g t", p=P, t=4))
        nc.scalar.dma_start(out=ac[1][:], in_=c.rearrange("(g p t) -> p g t", p=P, t=4))

        zc = [[keep.tile([P, 512], U32, name="zc%d%d" % (k, g), align_bytes=64) for g in range(2)] for k in range(4)]
        zs = [[keep.tile([P, 512], U8, name="zs%d%d" % (k, g), align_bytes=64) for g in range(2)] for k in range(4)]

        def z_transposes(g, k):
            words = zr[g][k][:].rearrange("p t k -> p (t k)").bitcast(F32)
            grouped = work.tile([P, 2048], BF16, tag="grouped", name="grouped", align_bytes=64)
            banks = []
            for half in range(2):
                bank = psum.tile([P, 2, 2, P], F32, tag="tr", name="ztr")
                for i in range(2):
                    base = 256 * (2 * half + i)
                    for e in range(2):
                        nc.tensor.transpose(bank[:, i, e, :], words[:, base + e : base + 256 : 2], ident[:])
                banks.append(bank)
            return grouped, banks

        def z_copies(state, engines=("s", "v")):
            grouped, banks = state
            for half in range(2):
                dst = grouped[:].bitcast(F32)[:, 512 * half : 512 * (half + 1)]
                dst = dst.rearrange("p (t r e) -> p t r e", t=2, e=2)
                src = banks[half][:].rearrange("p t e r -> p t r e")
                if engines[half] == "s":
                    nc.scalar.copy(out=dst, in_=src)
                else:
                    nc.vector.tensor_copy(out=dst, in_=src)

        def z_quant(state, g, k):
            nc.vector.quantize_mx(out=zc[k][g][:].bitcast(FP8X4), scales=zs[k][g][:], in_=state[0][:])

        sb = keep.tile([P, 32], F32, name="sb")

        def mx1(acc, j, g, k):
            cb, jj = j // 4, j % 4
            nc.tensor.matmul_mx(
                out=acc[:],
                lhsT=wt[cb][:, k, 256 * jj : 256 * (jj + 1)].bitcast(FP4X4),
                lhsT_scale=wsc[:, Z * k + P * j : Z * k + P * (j + 1)],
                rhs=zc[k][g][:].bitcast(FP8X4),
                rhs_scale=zs[k][g][:],
                start=(k == 0),
                stop=(k == 3),
            )

        def relu(acc, j):
            r = work.tile([P, 512], F32, tag="r", name="r", bufs=6)
            nc.scalar.activation(out=r[:], in_=acc[:], func=ACT.Relu, scale=sb[:, j : j + 1], bias=sb[:, 16 + j : 17 + j])
            return r

        def unit_a(g, j):
            acc = psum.tile([P, 512], F32, tag="acc", name="acc1")
            for k in range(4):
                mx1(acc, j, g, k)
            return relu(acc, j)

        def r_transposes(r):
            bank = psum.tile([P, 4, P], F32, tag="tr", name="rtr")
            for t in range(4):
                nc.tensor.transpose(bank[:, t, :], r[:, P * t : P * (t + 1)], ident[:])
            return bank

        def add_z(bank, g, j):
            h = work.tile([P, P, 4], F32, tag="h", name="h")
            col = P * (j % 4)
            nc.vector.tensor_tensor(
                out=h[:],
                in0=bank[:].rearrange("p t c -> p c t"),
                in1=zr[g][j // 4][:, :, col : col + P].rearrange("p t c -> p c t"),
                op=ALU.add,
            )
            return h

        def mul_a(h, x, g, j):
            jj = j % 4
            nc.vector.tensor_tensor(
                out=x[:, 512 * jj : 512 * (jj + 1)].rearrange("p (c t) -> p c t", t=4),
                in0=h[:],
                in1=ac[j // 8][:, g, :].unsqueeze(1).broadcast_to([P, P, 4]),
                op=ALU.mult,
            )

        xc = [[keep.tile([P, 512], U32, name="xc%d%d" % (cb, g), align_bytes=64) for g in range(2)] for cb in range(4)]
        xs = [[keep.tile([P, 512], U8, name="xs%d%d" % (cb, g), align_bytes=64) for g in range(2)] for cb in range(4)]

        def x_tile():
            return work.tile([P, 2048], BF16, tag="x", name="x", align_bytes=64, bufs=2)

        def quant_x(x, cb, g):
            nc.vector.quantize_mx(out=xc[cb][g][:].bitcast(FP8X4), scales=xs[cb][g][:], in_=x[:])

        def quant_unit(x, cb, g, jj):
            sl = slice(P * jj, P * (jj + 1))
            nc.vector.quantize_mx(
                out=xc[cb][g][:, sl].bitcast(FP8X4), scales=xs[cb][g][:, sl], in_=x[:, 512 * jj : 512 * (jj + 1)]
            )

        def e_mx(i):
            ub, jj = i // 4, i % 4
            sl = slice(P * jj, P * (jj + 1))
            accs = []
            for db in (2, 3):
                acc = psum.tile([P, 512], F32, tag="acc", name="acc2")
                for g in range(2):
                    nc.tensor.matmul_mx(
                        out=acc[:],
                        lhsT=xc[ub][g][:, sl].bitcast(FP8X4),
                        lhsT_scale=xs[ub][g][:, sl],
                        rhs=xc[db][g][:].bitcast(FP8X4),
                        rhs_scale=xs[db][g][:],
                        start=(g == 0),
                        stop=(g == 1),
                    )
                accs.append(acc)
            return accs

        def e_out(i, accs, engines):
            o = work.tile([P, 1024], F32, tag="o", name="o", bufs=4)
            for db in range(2):
                dst = o[:, 512 * db : 512 * (db + 1)]
                if engines[db] == "s":
                    nc.scalar.activation(out=dst, in_=accs[db][:], func=ACT.Copy, scale=1.0 / 32.0)
                else:
                    nc.vector.tensor_scalar(out=dst, in0=accs[db][:], scalar1=1.0 / 32.0, scalar2=None, op0=ALU.mult)
            nc.sync.dma_start(out=out_0[P * i : P * (i + 1), :], in_=o[:])
            return o

        def e_cast(o):
            ob = work.tile([P, 1024], BF16, tag="ob", name="ob", bufs=4)
            for db in range(2):
                sl = slice(512 * db, 512 * (db + 1))
                nc.vector.tensor_copy(
                    out=ob[:, sl].rearrange("r (e p l) -> r e p l", e=2, l=2),
                    in_=o[:, sl].rearrange("r (p e l) -> r e p l", e=2, l=2),
                )
            return ob

        def f_tr(ob):
            bank = psum.tile([P, 2, 2, P], F32, tag="tr", name="otr")
            words = ob[:].bitcast(F32)
            for db in range(2):
                for e in range(2):
                    col = 256 * db + P * e
                    nc.tensor.transpose(bank[:, db, e, :], words[:, col : col + P], ident[:])
            return bank

        def f_copy(bank, engine):
            y = work.tile([P, 1024], BF16, tag="y", name="y", align_bytes=64)
            dst = y[:].bitcast(F32).rearrange("p (d m e) -> p d m e", d=2, e=2)
            src = bank[:].rearrange("p d e m -> p d m e")
            if engine == "s":
                nc.scalar.copy(out=dst, in_=src)
            else:
                nc.vector.tensor_copy(out=dst, in_=src)
            return y

        yc = [keep.tile([P, 2, 256], U32, name="yc%d" % m, align_bytes=64) for m in range(4)]
        ys = [keep.tile([P, 2, 256], U8, name="ys%d" % m, align_bytes=64) for m in range(4)]

        def f_quant(y, i):
            sl = slice(P * (i % 2), P * (i % 2 + 1))
            for db in range(2):
                nc.vector.quantize_mx(
                    out=yc[i // 2][:, db, sl].bitcast(FP8X4),
                    scales=ys[i // 2][:, db, sl],
                    in_=y[:, 512 * db : 512 * (db + 1)],
                )

        def f_store(m):
            dst = out_1.rearrange("g p m t -> g p (m t)")[:, :, 1024 * m : 1024 * (m + 1)]
            nc.sync.dma_start(out=dst.bitcast(I32).rearrange("g p n -> p g n"), in_=yc[m][:].bitcast(I32))
            for q in range(4):
                nc.sync.dma_start(
                    out=out_2[:, 4 * q : 4 * q + 4, 256 * m : 256 * (m + 1)].bitcast(I32).rearrange("g r m -> r g m"),
                    in_=ys[m][32 * q : 32 * q + 4, :, :].bitcast(I32),
                )

        steps = [(2, 0), (3, 0), (2, 1), (3, 1), (0, 0), (0, 1), (1, 0), (1, 1)]

        zst = {}
        zst[0, 0] = z_transposes(0, 0)
        z_copies(zst[0, 0])
        zst[0, 1] = z_transposes(0, 1)
        z_quant(zst[0, 0], 0, 0)
        z_copies(zst[0, 1])
        rows_t = psum.tile([P, P], BF16, tag="tr", name="rows_t")
        nc.tensor.transpose(rows_t[:], rows[:], identb[:])
        nc.vector.tensor_copy(out=sb[:], in_=rows_t[:, 0:32])
        accs = []
        for i in range(4):
            acc = psum.tile([P, 512], F32, tag="acc", name="acc1")
            accs.append(acc)
        for k in range(4):
            if k > 0 and k < 3:
                zst[0, k + 1] = z_transposes(0, k + 1)
                z_quant(zst[0, k], 0, k)
                z_copies(zst[0, k + 1])
            elif k == 3:
                z_quant(zst[0, k], 0, k)
            for i in range(4):
                mx1(accs[i], 4 * steps[0][0] + i, 0, k)
        prev = [relu(accs[i], 4 * steps[0][0] + i) for i in range(4)]

        eo, eb, fb, fy = {}, {}, {}, {}
        for n in range(1, 8):
            cb, g = steps[n]
            pcb, pg = steps[n - 1]
            cur = []
            if n == 1:
                zst[1, 0] = z_transposes(1, 0)
                zst[1, 1] = z_transposes(1, 1)
                z_copies(zst[1, 0])
            cur.append(unit_a(g, 4 * cb))
            if n == 1:
                z_copies(zst[1, 1])
                z_quant(zst[1, 0], 1, 0)
            if n == 7:
                fb[0] = f_tr(eb[0])
                fb[1] = f_tr(eb[1])
            banks = [r_transposes(r) for r in prev]
            x = x_tile()
            h0 = add_z(banks[0], pg, 4 * pcb)
            h1 = add_z(banks[1], pg, 4 * pcb + 1)
            if n == 1:
                z_quant(zst[1, 1], 1, 1)
            cur.append(unit_a(g, 4 * cb + 1))
            if n == 7:
                fy[0] = f_copy(fb[0], "s")
                fy[1] = f_copy(fb[1], "s")
            mul_a(h0, x, pg, 4 * pcb)
            h2 = add_z(banks[2], pg, 4 * pcb + 2)
            if pcb < 2:
                quant_unit(x, pcb, pg, 0)
            if n == 1:
                zst[1, 2] = z_transposes(1, 2)
                zst[1, 3] = z_transposes(1, 3)
                z_copies(zst[1, 2])
            mul_a(h1, x, pg, 4 * pcb + 1)
            cur.append(unit_a(g, 4 * cb + 2))
            h3 = add_z(banks[3], pg, 4 * pcb + 3)
            if n == 1:
                z_quant(zst[1, 2], 1, 2)
                z_copies(zst[1, 3])
            if pcb < 2:
                quant_unit(x, pcb, pg, 1)
            mul_a(h2, x, pg, 4 * pcb + 2)
            if n == 7:
                banks = [r_transposes(r) for r in cur[0:2]]
            cur.append(unit_a(g, 4 * cb + 3))
            if n == 1:
                z_quant(zst[1, 3], 1, 3)
            if pcb < 2:
                quant_unit(x, pcb, pg, 2)
            mul_a(h3, x, pg, 4 * pcb + 3)
            if n == 6:
                for i in (0, 1):
                    ea = e_mx(i)
                    eo[i] = e_out(i, ea, "ss")
            if n == 7:
                f_quant(fy[0], 0)
                f_quant(fy[1], 1)
                f_store(0)
            if pcb < 2:
                quant_unit(x, pcb, pg, 3)
            else:
                quant_x(x, pcb, pg)
            if n == 6:
                eb[0] = e_cast(eo[0])
                eb[1] = e_cast(eo[1])
            prev = cur

        x = x_tile()
        for i in (2, 3):
            ea = e_mx(i)
            eo[i] = e_out(i, ea, "ss")
        h0 = add_z(banks[0], 1, 4)
        h1 = add_z(banks[1], 1, 5)
        mul_a(h0, x, 1, 4)
        mul_a(h1, x, 1, 5)
        quant_unit(x, 1, 1, 0)
        banks = [r_transposes(r) for r in prev[2:4]]
        eb[2] = e_cast(eo[2])
        eb[3] = e_cast(eo[3])
        quant_unit(x, 1, 1, 1)
        h2 = add_z(banks[0], 1, 6)
        h3 = add_z(banks[1], 1, 7)
        fb[2] = f_tr(eb[2])
        fb[3] = f_tr(eb[3])
        fy[2] = f_copy(fb[2], "s")
        fy[3] = f_copy(fb[3], "s")
        mul_a(h2, x, 1, 6)
        mul_a(h3, x, 1, 7)
        for i in (4, 5):
            ea = e_mx(i)
            eo[i] = e_out(i, ea, "ss")
        quant_unit(x, 1, 1, 2)
        f_quant(fy[2], 2)
        quant_unit(x, 1, 1, 3)
        f_quant(fy[3], 3)
        f_store(1)
        for i in (6, 7):
            ea = e_mx(i)
            eo[i] = e_out(i, ea, "sv")
        eb[4] = e_cast(eo[4])
        eb[5] = e_cast(eo[5])
        fb[4] = f_tr(eb[4])
        fb[5] = f_tr(eb[5])
        fy[4] = f_copy(fb[4], "s")
        fy[5] = f_copy(fb[5], "v")
        eb[6] = e_cast(eo[6])
        eb[7] = e_cast(eo[7])
        f_quant(fy[4], 4)
        f_quant(fy[5], 5)
        f_store(2)
        fb[6] = f_tr(eb[6])
        fb[7] = f_tr(eb[7])
        fy[6] = f_copy(fb[6], "s")
        fy[7] = f_copy(fb[7], "v")
        f_quant(fy[6], 6)
        f_quant(fy[7], 7)
        f_store(3)
